import numpy as np
import ml_dtypes


def mxq(x, axis, fmt="e4m3"):
    dtype, down = {"e4m3": (ml_dtypes.float8_e4m3fn, 7), "e5m2": (ml_dtypes.float8_e5m2, 14)}[fmt]
    v = np.moveaxis(np.asarray(x, np.float32).astype(ml_dtypes.bfloat16).astype(np.float64), axis, -1)
    blocks = v.reshape(v.shape[:-1] + (-1, 32))
    amax = np.abs(blocks).max(-1, keepdims=True)
    byte = np.maximum(np.where(amax > 0, np.frexp(amax)[1] - 1 + 127, 0) - down, 1)
    scale = np.exp2(byte - 127.0)
    codes = (blocks / scale).astype(np.float32).astype(dtype).astype(np.float64)
    return np.moveaxis((codes * scale).reshape(v.shape), -1, axis)


WIDE = False


def mx_kscale(k):
    if not WIDE:
        return np.ones(k)
    levels = np.array([10, -10, 5, -5, 0])
    if k % 512:
        return np.exp2(np.random.permutation(np.resize(levels, k // 32))).repeat(32)
    a = np.empty((k // 512, 16))
    for p in range(k // 512):
        a[p, :8] = np.random.permutation(np.resize(levels, 8))
        for g in range(8):
            far = levels[np.abs(levels - a[p, g]) >= 10]
            a[p, g + 8] = far[np.random.randint(len(far))]
    return np.exp2(a.ravel()).repeat(32)


def f64(x):
    return np.asarray(x).astype(np.float64)


def striped(idx):
    return np.tile(idx.reshape(-1, 16).T, (8, 1)).astype(np.uint16)


def unstriped(offs):
    return offs[:16].T.reshape(-1).astype(np.int64)


E2M1 = np.array([0.0, 0.5, 1.0, 1.5, 2.0, 3.0, 4.0, 6.0, -0.0, -0.5, -1.0, -1.5, -2.0, -3.0, -4.0, -6.0])


def pack_weight(w, fmt):
    k, n = w.shape
    w = f64(np.asarray(w, np.float32).astype(ml_dtypes.bfloat16)).reshape(k // 32, 32, n)
    amax = np.abs(w).max(1)
    if fmt == "e4m3":
        byte = np.frexp(amax)[1] - 1 + 127 - 7
    else:
        mant, ex = np.frexp(amax / 6.0)
        byte = np.where(mant > 0.5, ex, ex - 1) + 127
    byte = np.clip(np.where(amax > 0, byte, 1), 1, 254)
    scaled = (w * np.exp2(127.0 - byte)[:, None, :]).reshape(k, n).astype(np.float32)
    by_word = np.ascontiguousarray(scaled.reshape(k // 512, 128, 4, n).transpose(0, 1, 3, 2))
    if fmt == "e4m3":
        words = by_word.astype(ml_dtypes.float8_e4m3fn).view(np.uint8)
    else:
        c = by_word.astype(ml_dtypes.float4_e2m1fn).view(np.uint8) & 0xF
        words = (c[..., 0::2] | (c[..., 1::2] << 4)).reshape(k // 512, 128, 2 * n)
    return np.ascontiguousarray(words), np.ascontiguousarray(byte.astype(np.uint8).reshape(k // 512, 16, n))


def unpack_weight(words, scales, fmt):
    g, _, n = scales.shape
    words = np.ascontiguousarray(words).reshape(g, 128, n, -1)
    if fmt == "e4m3":
        vals = words.view(ml_dtypes.float8_e4m3fn).astype(np.float64)
    else:
        nib = np.empty((g, 128, n, 4), np.uint8)
        nib[..., 0::2] = words & 0xF
        nib[..., 1::2] = words >> 4
        vals = E2M1[nib]
    vals = vals * np.repeat(np.exp2(scales.astype(np.float64) - 127.0), 8, axis=1)[..., None]
    return vals.transpose(0, 1, 3, 2).reshape(g * 512, n)


def gelu(v):
    return 0.5 * v * (1.0 + np.tanh(np.sqrt(2.0 / np.pi) * (v + 0.044715 * v**3)))


K, T, S, H, T3, S2, T2 = 1024, 2048, 1024, 1024, 2048, 512, 2048

def setup_inputs():
    n = np.random.standard_normal
    s = mx_kscale(K)[:, None]
    u = mx_kscale(H)[:, None]
    tab_words, tab_scales = pack_weight(n((K, T)) * s, "e4m3")
    tab2_words, tab2_scales = pack_weight(n((H, T3)) / np.sqrt(H) / u, "e4m3")
    w2_words, w2_scales = pack_weight(0.8 * n((K, H)) / np.sqrt(K) / s * u.T, "e2m1")
    return {
        "tab_words": tab_words, "tab_scales": tab_scales,
        "offs": striped(np.random.permutation(T)[:S]),
        "tab2_words": tab2_words, "tab2_scales": tab2_scales,
        "offs2": striped(np.random.permutation(T3)[:S2]),
        "offs3": striped(np.random.permutation(T2)[:S]),
        "w1": (1.5 * n((K, H)) / np.sqrt(K) / s).astype(np.float32),
        "w2_words": w2_words, "w2_scales": w2_scales,
        "gain": (1.3 * np.exp(0.3 * n(H)) * u[:, 0]).astype(np.float32),
        "least": ((0.8 * n((H, S)) - 0.5) * u).astype(np.float32),
        "peer": np.exp(0.4 * n(S2)).astype(np.float32),
        "cap": (0.4 + 0.5 * n(S2)).astype(np.float32),
        "wgo": np.exp(0.3 * n((128, S))).astype(np.float32),
        "page1": n((S2, T2)).astype(np.float32),
    }

def reference(tab_words, tab_scales, offs, tab2_words, tab2_scales, offs2, offs3,
              w1, w2_words, w2_scales, gain, least, peer, cap, wgo, page1):
    v = unpack_weight(tab_words, tab_scales, "e4m3")[:, unstriped(offs)]
    v2 = unpack_weight(tab2_words, tab2_scales, "e4m3")[:, unstriped(offs2)]
    w2 = unpack_weight(w2_words, w2_scales, "e2m1")
    x = mxq(f64(w1), 0, "e4m3").T @ v
    d = w2.T @ v
    h = np.maximum(f64(gain)[:, None] * np.tanh(x) + d, f64(least))
    e = v2.T @ mxq(h, 0, "e4m3")
    y = np.minimum(f64(peer)[:, None] * e, f64(cap)[:, None])
    out = f64(page1).copy()
    out[:, unstriped(offs3)] = np.tile(f64(wgo), (S2 // 128, 1)) * y
    return out

@@ -1,0 +1,292 @@
+from contextlib import ExitStack
+
+import concourse.mybir as mybir
+
+K, T, S, H, T3, S2, T2 = 1024, 2048, 1024, 1024, 2048, 512, 2048
+FLOPS = 2 * K * H * S * 2 + 2 * H * S2 * S
+
+F32 = mybir.dt.float32
+BF16 = mybir.dt.bfloat16
+I32 = mybir.dt.int32
+U32 = mybir.dt.uint32
+U16 = mybir.dt.uint16
+U8 = mybir.dt.uint8
+FP8X4 = mybir.dt.float8_e4m3fn_x4
+FP4X4 = mybir.dt.float4_e2m1fn_x4
+ALU = mybir.AluOpType
+ACT = mybir.ActivationFunctionType
+
+P = 128
+PACK = 4
+PASS = P * PACK
+QUADS = 4
+NJ = 512
+
+
+def tile_list_league_page_scores_kernel(
+    tc, tab_words, tab_scales, offs, tab2_words, tab2_scales, offs2, offs3,
+    w1, w2_words, w2_scales, gain, least, peer, cap, wgo, page1, out,
+):
+    nc = tc.nc
+    k_passes = K // PASS
+    r_passes = H // PASS
+    j_chunks = S // NJ
+    m_tiles = S2 // P
+
+    with ExitStack() as ctx:
+        keep = ctx.enter_context(tc.tile_pool(name="keep", bufs=1))
+        ring = ctx.enter_context(tc.tile_pool(name="ring", bufs=2))
+        psum = ctx.enter_context(tc.psum_pool(name="psum", bufs=1))
+
+        def held(shape, dtype, name):
+            return keep.tile(shape, dtype, name=name, align_bytes=64)
+
+        def streamed(shape, dtype):
+            return ring.tile(shape, dtype, name="stream", bufs=4, align_bytes=64)
+
+        def load_words(table, a):
+            words = streamed([P, table.shape[2]], I32)
+            nc.sync.dma_start(out=words[:], in_=table[a].rearrange("p t i -> p (t i)").bitcast(I32))
+            return words
+
+        def load_packed_scales(queue, plane, scales):
+            for q in range(QUADS):
+                queue.dma_start(
+                    out=plane[32 * q : 32 * q + 8, :].bitcast(I32),
+                    in_=scales[:, 4 * q : 4 * q + 4, :].bitcast(I32),
+                )
+
+        w1_raw = {}
+
+        def load_w1(a, b):
+            raw = streamed([P, PACK, PASS], F32)
+            nc.sync.dma_start(
+                out=raw[:],
+                in_=w1[a * PASS : (a + 1) * PASS, b * PASS : (b + 1) * PASS].rearrange("(p i) c -> p i c", i=PACK),
+            )
+            w1_raw[a, b] = raw
+
+        least_sb = {}
+
+        def load_least(b, jc):
+            rows = streamed([P, PACK, NJ], F32)
+            nc.sync.dma_start(
+                out=rows[:],
+                in_=least[b * PASS : (b + 1) * PASS, jc * NJ : (jc + 1) * NJ].rearrange("(p t) j -> p t j", t=PACK),
+            )
+            least_sb[b, jc] = rows
+
+        def load_list(source, name):
+            entries = held(list(source.shape), U16, name)
+            nc.sync.dma_start(out=entries[:], in_=source)
+            return entries
+
+        tab_rows = held([P, T], U8, "tab_rows")
+        load_packed_scales(nc.sync, tab_rows, tab_scales)
+        idx = load_list(offs, "idx")
+        tab_sb = [load_words(tab_words, 0)]
+        load_w1(0, 0)
+        w2_raw = held([P, k_passes, H // 2], I32, "w2_raw")
+        nc.sync.dma_start(out=w2_raw[:], in_=w2_words.rearrange("a p c -> p a c").bitcast(I32))
+        load_w1(1, 0)
+        tab_sb.append(load_words(tab_words, 1))
+        idx2 = load_list(offs2, "idx2")
+        idx3 = load_list(offs3, "idx3")
+
+        w2_plane_raw = held([P, k_passes, H], U8, "raw_plane")
+        nc.gpsimd.memset(w2_plane_raw[:].rearrange("p a c -> p (a c)").bitcast(I32), 0)
+        for q in range(QUADS):
+            nc.gpsimd.dma_start(
+                out=w2_plane_raw[32 * q : 32 * q + 4, :, :].bitcast(I32),
+                in_=w2_scales[:, 4 * q : 4 * q + 4, :].rearrange("a r c -> r a c").bitcast(I32),
+            )
+        gain_sb = held([P, r_passes, PACK], F32, "gain_sb")
+        nc.gpsimd.dma_start(out=gain_sb[:], in_=gain.rearrange("(b p t) -> p b t", p=P, t=PACK))
+
+        tab_plane = held([P, T], U8, "tab_plane")
+        nc.vector.memset(tab_plane[:].bitcast(I32), 0)
+        v_plane1 = held([P, S], U8, "v_plane1")
+        nc.vector.memset(v_plane1[:].bitcast(I32), 0)
+        for q in range(QUADS):
+            live = slice(32 * q, 32 * q + 8)
+            nc.vector.tensor_copy(out=tab_plane[live, :].bitcast(I32), in_=tab_rows[live, :].bitcast(I32))
+        v_plane = held([P, S], U8, "v_plane")
+        nc.vector.tensor_copy(out=v_plane[:], in_=tab_plane[:].indirect(idx[:]))
+        for q in range(QUADS):
+            nc.sync.dma_start(
+                out=v_plane1[32 * q : 32 * q + 4, :].bitcast(I32),
+                in_=v_plane[32 * q + 4 : 32 * q + 8, :].bitcast(I32),
+            )
+
+        v_codes = {}
+
+        def gather_v(a, jc):
+            codes = held([P, NJ], U32, "v_codes%d%d" % (a, jc))
+            cols = slice(jc * NJ // 16, (jc + 1) * NJ // 16)
+            nc.vector.tensor_copy(out=codes[:], in_=tab_sb[a][:].bitcast(U32).indirect(idx[:, cols]))
+            v_codes[a, jc] = codes
+
+        w2_codes = held([P, k_passes * r_passes, PACK, P], U16, "w2_codes")
+        w2_plane = held([P, k_passes * r_passes, PACK, P], U8, "w2_plane")
+
+        def deal_w2():
+            nc.vector.tensor_copy(
+                out=w2_codes[:],
+                in_=w2_raw[:].rearrange("p a c -> p (a c)").bitcast(U16).rearrange("p (g m t) -> p g t m", t=PACK, m=P),
+            )
+            nc.vector.tensor_copy(
+                out=w2_plane[:],
+                in_=w2_plane_raw[:].rearrange("p a (b m t) -> p (a b) t m", t=PACK, m=P),
+            )
+
+        w1_codes = {}
+        w1_plane = {}
+
+        def quantise_w1(a, b):
+            grouped = ring.tile([P, PACK, P, PACK], BF16, name="w1_grouped", align_bytes=64)
+            nc.scalar.copy(
+                out=grouped[:].rearrange("p t m i -> p m i t"),
+                in_=w1_raw[a, b][:].rearrange("p i (m t) -> p m i t", t=PACK),
+            )
+            codes = held([P, PASS], U32, "w1_codes%d%d" % (a, b))
+            plane = held([P, PASS], U8, "w1_plane%d%d" % (a, b))
+            nc.vector.quantize_mx(
+                out=codes[:].bitcast(FP8X4), scales=plane[:], in_=grouped[:].rearrange("p t m i -> p (t m i)")
+            )
+            w1_codes[a, b] = codes
+            w1_plane[a, b] = plane
+
+        h_codes = {}
+        h_plane = {}
+
+        def features(b, jc):
+            cols = slice(jc * NJ, (jc + 1) * NJ)
+            u = ring.tile([P, PACK, NJ], F32, name="u")
+            for t in range(PACK):
+                ch = slice(t * P, (t + 1) * P)
+                x_ps = psum.tile([P, NJ], F32, name="x_ps", bufs=3)
+                d_ps = psum.tile([P, NJ], F32, name="d_ps", bufs=3)
+                for a in range(k_passes):
+                    nc.tensor.matmul_mx(
+                        out=x_ps[:],
+                        lhsT=w1_codes[a, b][:, ch].bitcast(FP8X4),
+                        lhsT_scale=w1_plane[a, b][:, ch],
+                        rhs=v_codes[a, jc][:].bitcast(FP8X4),
+                        rhs_scale=v_plane[4 * a : P, cols],
+                        start=(a == 0),
+                        stop=(a == k_passes - 1),
+                    )
+                for a in range(k_passes):
+                    g = a * r_passes + b
+                    nc.tensor.matmul_mx(
+                        out=d_ps[:],
+                        lhsT=w2_codes[:, g, t, :].bitcast(FP4X4),
+                        lhsT_scale=w2_plane[:, g, t, :],
+                        rhs=v_codes[a, jc][:].bitcast(FP8X4),
+                        rhs_scale=(v_plane, v_plane1)[a][:, cols],
+                        start=(a == 0),
+                        stop=(a == k_passes - 1),
+                    )
+                bent = ring.tile([P, NJ], F32, name="bent", bufs=4)
+                nc.scalar.activation(out=bent[:], in_=x_ps[:], func=ACT.Tanh)
+                nc.vector.scalar_tensor_tensor(
+                    out=u[:, t, :], in0=bent[:], scalar=gain_sb[:, b, t : t + 1], in1=d_ps[:],
+                    op0=ALU.mult, op1=ALU.add,
+                )
+            grouped = ring.tile([P, NJ, PACK], BF16, name="h_grouped", align_bytes=64)
+            nc.vector.tensor_tensor(
+                out=grouped[:].rearrange("p (c i) t -> p c t i", i=4),
+                in0=u[:].rearrange("p t (c i) -> p c t i", i=4),
+                in1=least_sb[b, jc][:].rearrange("p t (c i) -> p c t i", i=4),
+                op=ALU.max,
+            )
+            codes = held([P, NJ], U32, "h_codes%d%d" % (b, jc))
+            plane = held([P, NJ], U8, "h_plane%d%d" % (b, jc))
+            nc.vector.quantize_mx(
+                out=codes[:].bitcast(FP8X4), scales=plane[:], in_=grouped[:].rearrange("p j t -> p (j t)")
+            )
+            h_codes[b, jc] = codes
+            h_plane[b, jc] = plane
+
+        v2_codes = []
+        v2_plane = held([P, S2], U8, "v2_plane")
+
+        def gather_v2(tab2_plane, tab2_sb, idx2):
+            nc.vector.tensor_copy(out=v2_plane[:], in_=tab2_plane[:].indirect(idx2[:]))
+            for b in range(r_passes):
+                codes = held([P, S2], U32, "v2_codes%d" % b)
+                nc.vector.tensor_copy(out=codes[:], in_=tab2_sb[b][:].bitcast(U32).indirect(idx2[:]))
+                v2_codes.append(codes)
+
+        def scores(mb, jc, page):
+            peers = slice(mb * P, (mb + 1) * P)
+            e_ps = psum.tile([P, NJ], F32, name="e_ps", bufs=2)
+            for b in range(r_passes):
+                nc.tensor.matmul_mx(
+                    out=e_ps[:],
+                    lhsT=v2_codes[b][:, peers].bitcast(FP8X4),
+                    lhsT_scale=v2_plane[4 * b : P, peers],
+                    rhs=h_codes[b, jc][:].bitcast(FP8X4),
+                    rhs_scale=h_plane[b, jc][:],
+                    start=(b == 0),
+                    stop=(b == r_passes - 1),
+                )
+            e_sb = ring.tile([P, NJ], F32, name="e_sb", bufs=3)
+            nc.scalar.copy(out=e_sb[:], in_=e_ps[:])
+            capped = ring.tile([P, NJ], F32, name="capped")
+            nc.vector.tensor_scalar(
+                out=capped[:], in0=e_sb[:], scalar1=limits[:, 0, mb : mb + 1], scalar2=limits[:, 1, mb : mb + 1],
+                op0=ALU.mult, op1=ALU.min,
+            )
+            nc.vector.tensor_tensor(
+                out=page[:].indirect(idx3[:, jc * NJ // 16 : (jc + 1) * NJ // 16]),
+                in0=capped[:],
+                in1=wgo_sb[:, jc * NJ : (jc + 1) * NJ],
+                op=ALU.mult,
+            )
+
+        gather_v(0, 0)
+        gather_v(0, 1)
+        load_least(0, 0)
+        deal_w2()
+        quantise_w1(0, 0)
+        load_w1(0, 1)
+        gather_v(1, 0)
+        quantise_w1(1, 0)
+        load_w1(1, 1)
+        gather_v(1, 1)
+        load_least(0, 1)
+        tab2_plane = held([P, T3], U8, "raw_plane")
+        nc.gpsimd.memset(tab2_plane[:].bitcast(I32), 0)
+        load_packed_scales(nc.sync, tab2_plane, tab2_scales)
+        limits = held([P, 2, 8], F32, "w2_raw")
+        with nc.allow_non_contiguous_dma("one value of a short vector to each partition"):
+            nc.sync.dma_start(out=limits[:, 0, 0:m_tiles], in_=peer.rearrange("(mb p) -> p mb", p=P))
+            nc.sync.dma_start(out=limits[:, 1, 0:m_tiles], in_=cap.rearrange("(mb p) -> p mb", p=P))
+        features(0, 0)
+        load_least(1, 0)
+        quantise_w1(0, 1)
+        tab2_sb = [load_words(tab2_words, 0)]
+        quantise_w1(1, 1)
+        tab2_sb.append(load_words(tab2_words, 1))
+        features(0, 1)
+        load_least(1, 1)
+        wgo_sb = ring.tile([P, S], F32, name="w1_grouped", align_bytes=64)
+        nc.sync.dma_start(out=wgo_sb[:], in_=wgo)
+        features(1, 0)
+
+        def load_page(mb):
+            page = streamed([P, T2], F32)
+            nc.sync.dma_start(out=page[:], in_=page1[mb * P : (mb + 1) * P, :])
+            return page
+
+        pages = [load_page(0)]
+        gather_v2(tab2_plane, tab2_sb, idx2)
+        pages.append(load_page(1))
+        pages.append(load_page(2))
+        features(1, 1)
+        pages.append(load_page(3))
+        for mb in range(m_tiles):
+            for jc in range(j_chunks):
+                scores(mb, jc, pages[mb])
+            nc.sync.dma_start(out=out[mb * P : (mb + 1) * P, :], in_=pages[mb][:])

@@ -42,7 +42,7 @@ def tile_list_league_page_scores_kernel(
             return keep.tile(shape, dtype, name=name, align_bytes=64)
 
         def streamed(shape, dtype):
-            return ring.tile(shape, dtype, name="stream", bufs=4, align_bytes=64)
+            return ring.tile(shape, dtype, name="stream", bufs=6, align_bytes=64)
 
         def load_words(table, a):
             words = streamed([P, table.shape[2]], I32)
@@ -66,6 +66,16 @@ def tile_list_league_page_scores_kernel(
             )
             w1_raw[a, b] = raw
 
+        w2_raw = {}
+
+        def load_w2(b):
+            raw = streamed([P, k_passes, PASS // 2], I32)
+            nc.sync.dma_start(
+                out=raw[:],
+                in_=w2_words[:, :, 2 * b * PASS : 2 * (b + 1) * PASS].rearrange("a p c -> p a c").bitcast(I32),
+            )
+            w2_raw[b] = raw
+
         least_sb = {}
 
         def load_least(b, jc):
@@ -81,42 +91,36 @@ def tile_list_league_page_scores_kernel(
             nc.sync.dma_start(out=entries[:], in_=source)
             return entries
 
+        w2_plane_raw = held([P, k_passes, H], U8, "raw_plane")
+        nc.gpsimd.memset(w2_plane_raw[:].rearrange("p a c -> p (a c)").bitcast(I32), 0)
+        tab_plane = streamed([P, T], U8)
+        nc.vector.memset(tab_plane[:].bitcast(I32), 0)
         tab_rows = held([P, T], U8, "tab_rows")
         load_packed_scales(nc.sync, tab_rows, tab_scales)
         idx = load_list(offs, "idx")
         tab_sb = [load_words(tab_words, 0)]
         load_w1(0, 0)
-        w2_raw = held([P, k_passes, H // 2], I32, "w2_raw")
-        nc.sync.dma_start(out=w2_raw[:], in_=w2_words.rearrange("a p c -> p a c").bitcast(I32))
-        load_w1(1, 0)
-        tab_sb.append(load_words(tab_words, 1))
-        idx2 = load_list(offs2, "idx2")
-        idx3 = load_list(offs3, "idx3")
-
-        w2_plane_raw = held([P, k_passes, H], U8, "raw_plane")
-        nc.gpsimd.memset(w2_plane_raw[:].rearrange("p a c -> p (a c)").bitcast(I32), 0)
+        load_w2(0)
         for q in range(QUADS):
-            nc.gpsimd.dma_start(
+            nc.sync.dma_start(
                 out=w2_plane_raw[32 * q : 32 * q + 4, :, :].bitcast(I32),
                 in_=w2_scales[:, 4 * q : 4 * q + 4, :].rearrange("a r c -> r a c").bitcast(I32),
             )
+        load_w1(1, 0)
+        tab_sb.append(load_words(tab_words, 1))
         gain_sb = held([P, r_passes, PACK], F32, "gain_sb")
         nc.gpsimd.dma_start(out=gain_sb[:], in_=gain.rearrange("(b p t) -> p b t", p=P, t=PACK))
+        idx2 = load_list(offs2, "idx2")
+        idx3 = load_list(offs3, "idx3")
 
-        tab_plane = held([P, T], U8, "tab_plane")
-        nc.vector.memset(tab_plane[:].bitcast(I32), 0)
         v_plane1 = held([P, S], U8, "v_plane1")
-        nc.vector.memset(v_plane1[:].bitcast(I32), 0)
+        nc.gpsimd.memset(v_plane1[:].bitcast(I32), 0)
         for q in range(QUADS):
             live = slice(32 * q, 32 * q + 8)
             nc.vector.tensor_copy(out=tab_plane[live, :].bitcast(I32), in_=tab_rows[live, :].bitcast(I32))
         v_plane = held([P, S], U8, "v_plane")
         nc.vector.tensor_copy(out=v_plane[:], in_=tab_plane[:].indirect(idx[:]))
-        for q in range(QUADS):
-            nc.sync.dma_start(
-                out=v_plane1[32 * q : 32 * q + 4, :].bitcast(I32),
-                in_=v_plane[32 * q + 4 : 32 * q + 8, :].bitcast(I32),
-            )
+        nc.sync.dma_start(out=v_plane1[0:100, :].bitcast(I32), in_=v_plane[4:104, :].bitcast(I32))
 
         v_codes = {}
 
@@ -126,18 +130,22 @@ def tile_list_league_page_scores_kernel(
             nc.vector.tensor_copy(out=codes[:], in_=tab_sb[a][:].bitcast(U32).indirect(idx[:, cols]))
             v_codes[a, jc] = codes
 
-        w2_codes = held([P, k_passes * r_passes, PACK, P], U16, "w2_codes")
-        w2_plane = held([P, k_passes * r_passes, PACK, P], U8, "w2_plane")
+        w2_codes = {}
+        w2_plane = {}
 
-        def deal_w2():
+        def deal_w2(b):
+            codes = held([P, k_passes, PACK, P], U16, "w2_codes%d" % b)
+            plane = held([P, k_passes, PACK, P], U8, "w2_plane%d" % b)
             nc.vector.tensor_copy(
-                out=w2_codes[:],
-                in_=w2_raw[:].rearrange("p a c -> p (a c)").bitcast(U16).rearrange("p (g m t) -> p g t m", t=PACK, m=P),
+                out=codes[:],
+                in_=w2_raw[b][:].rearrange("p a c -> p (a c)").bitcast(U16).rearrange("p (a m t) -> p a t m", t=PACK, m=P),
             )
             nc.vector.tensor_copy(
-                out=w2_plane[:],
-                in_=w2_plane_raw[:].rearrange("p a (b m t) -> p (a b) t m", t=PACK, m=P),
+                out=plane[:],
+                in_=w2_plane_raw[:, :, b * PASS : (b + 1) * PASS].rearrange("p a (m t) -> p a t m", t=PACK),
             )
+            w2_codes[b] = codes
+            w2_plane[b] = plane
 
         w1_codes = {}
         w1_plane = {}
@@ -159,47 +167,32 @@ def tile_list_league_page_scores_kernel(
         h_codes = {}
         h_plane = {}
 
-        def features(b, jc):
+        def products(b, t, jc, x_ps, d_ps, bent):
             cols = slice(jc * NJ, (jc + 1) * NJ)
-            u = ring.tile([P, PACK, NJ], F32, name="u")
-            for t in range(PACK):
-                ch = slice(t * P, (t + 1) * P)
-                x_ps = psum.tile([P, NJ], F32, name="x_ps", bufs=3)
-                d_ps = psum.tile([P, NJ], F32, name="d_ps", bufs=3)
-                for a in range(k_passes):
-                    nc.tensor.matmul_mx(
-                        out=x_ps[:],
-                        lhsT=w1_codes[a, b][:, ch].bitcast(FP8X4),
-                        lhsT_scale=w1_plane[a, b][:, ch],
-                        rhs=v_codes[a, jc][:].bitcast(FP8X4),
-                        rhs_scale=v_plane[4 * a : P, cols],
-                        start=(a == 0),
-                        stop=(a == k_passes - 1),
-                    )
-                for a in range(k_passes):
-                    g = a * r_passes + b
-                    nc.tensor.matmul_mx(
-                        out=d_ps[:],
-                        lhsT=w2_codes[:, g, t, :].bitcast(FP4X4),
-                        lhsT_scale=w2_plane[:, g, t, :],
-                        rhs=v_codes[a, jc][:].bitcast(FP8X4),
-                        rhs_scale=(v_plane, v_plane1)[a][:, cols],
-                        start=(a == 0),
-                        stop=(a == k_passes - 1),
-                    )
-                bent = ring.tile([P, NJ], F32, name="bent", bufs=4)
-                nc.scalar.activation(out=bent[:], in_=x_ps[:], func=ACT.Tanh)
-                nc.vector.scalar_tensor_tensor(
-                    out=u[:, t, :], in0=bent[:], scalar=gain_sb[:, b, t : t + 1], in1=d_ps[:],
-                    op0=ALU.mult, op1=ALU.add,
+            ch = slice(t * P, (t + 1) * P)
+            for a in range(k_passes):
+                nc.tensor.matmul_mx(
+                    out=x_ps[:],
+                    lhsT=w1_codes[a, b][:, ch].bitcast(FP8X4),
+                    lhsT_scale=w1_plane[a, b][:, ch],
+                    rhs=v_codes[a, jc][:].bitcast(FP8X4),
+                    rhs_scale=v_plane[4 * a : P, cols],
+                    start=(a == 0),
+                    stop=(a == k_passes - 1),
                 )
-            grouped = ring.tile([P, NJ, PACK], BF16, name="h_grouped", align_bytes=64)
-            nc.vector.tensor_tensor(
-                out=grouped[:].rearrange("p (c i) t -> p c t i", i=4),
-                in0=u[:].rearrange("p t (c i) -> p c t i", i=4),
-                in1=least_sb[b, jc][:].rearrange("p t (c i) -> p c t i", i=4),
-                op=ALU.max,
-            )
+            for a in range(k_passes):
+                nc.tensor.matmul_mx(
+                    out=d_ps[:],
+                    lhsT=w2_codes[b][:, a, t, :].bitcast(FP4X4),
+                    lhsT_scale=w2_plane[b][:, a, t, :],
+                    rhs=v_codes[a, jc][:].bitcast(FP8X4),
+                    rhs_scale=(v_plane, v_plane1)[a][:, cols],
+                    start=(a == 0),
+                    stop=(a == k_passes - 1),
+                )
+            nc.scalar.activation(out=bent[:], in_=x_ps[:], func=ACT.Tanh)
+
+        def quantise_h(b, jc, grouped):
             codes = held([P, NJ], U32, "h_codes%d%d" % (b, jc))
             plane = held([P, NJ], U8, "h_plane%d%d" % (b, jc))
             nc.vector.quantize_mx(
@@ -207,6 +200,29 @@ def tile_list_league_page_scores_kernel(
             )
             h_codes[b, jc] = codes
             h_plane[b, jc] = plane
+
+        def floor_and_round(out_rows, sums, floor_rows):
+            nc.vector.tensor_tensor(
+                out=out_rows.rearrange("p (c i) t -> p c t i", i=4),
+                in0=sums.rearrange("p t (c i) -> p c t i", i=4),
+                in1=floor_rows.rearrange("p t (c i) -> p c t i", i=4),
+                op=ALU.max,
+            )
+
+        def features_on_vector(b, jc):
+            u = ring.tile([P, PACK, NJ], F32, name="u")
+            for t in range(PACK):
+                x_ps = psum.tile([P, NJ], F32, name="x_ps", bufs=3)
+                d_ps = psum.tile([P, NJ], F32, name="d_ps", bufs=3)
+                bent = ring.tile([P, NJ], F32, name="bent", bufs=4)
+                products(b, t, jc, x_ps, d_ps, bent)
+                nc.vector.scalar_tensor_tensor(
+                    out=u[:, t, :], in0=bent[:], scalar=gain_sb[:, b, t : t + 1], in1=d_ps[:],
+                    op0=ALU.mult, op1=ALU.add,
+                )
+            grouped = ring.tile([P, NJ, PACK], BF16, name="h_grouped", align_bytes=64)
+            floor_and_round(grouped[:], u[:], least_sb[b, jc][:])
+            quantise_h(b, jc, grouped)
 
         v2_codes = []
         v2_plane = held([P, S2], U8, "v2_plane")
@@ -231,7 +247,7 @@ def tile_list_league_page_scores_kernel(
                     start=(b == 0),
                     stop=(b == r_passes - 1),
                 )
-            e_sb = ring.tile([P, NJ], F32, name="e_sb", bufs=3)
+            e_sb = ring.tile([P, NJ], F32, name="e_sb", bufs=8)
             nc.scalar.copy(out=e_sb[:], in_=e_ps[:])
             capped = ring.tile([P, NJ], F32, name="capped")
             nc.vector.tensor_scalar(
@@ -245,47 +261,48 @@ def tile_list_league_page_scores_kernel(
                 op=ALU.mult,
             )
 
-        gather_v(0, 0)
-        gather_v(0, 1)
-        load_least(0, 0)
-        deal_w2()
-        quantise_w1(0, 0)
-        load_w1(0, 1)
-        gather_v(1, 0)
-        quantise_w1(1, 0)
-        load_w1(1, 1)
-        gather_v(1, 1)
-        load_least(0, 1)
-        tab2_plane = held([P, T3], U8, "raw_plane")
-        nc.gpsimd.memset(tab2_plane[:].bitcast(I32), 0)
-        load_packed_scales(nc.sync, tab2_plane, tab2_scales)
-        limits = held([P, 2, 8], F32, "w2_raw")
-        with nc.allow_non_contiguous_dma("one value of a short vector to each partition"):
-            nc.sync.dma_start(out=limits[:, 0, 0:m_tiles], in_=peer.rearrange("(mb p) -> p mb", p=P))
-            nc.sync.dma_start(out=limits[:, 1, 0:m_tiles], in_=cap.rearrange("(mb p) -> p mb", p=P))
-        features(0, 0)
-        load_least(1, 0)
-        quantise_w1(0, 1)
-        tab2_sb = [load_words(tab2_words, 0)]
-        quantise_w1(1, 1)
-        tab2_sb.append(load_words(tab2_words, 1))
-        features(0, 1)
-        load_least(1, 1)
-        wgo_sb = ring.tile([P, S], F32, name="w1_grouped", align_bytes=64)
-        nc.sync.dma_start(out=wgo_sb[:], in_=wgo)
-        features(1, 0)
-
         def load_page(mb):
             page = streamed([P, T2], F32)
             nc.sync.dma_start(out=page[:], in_=page1[mb * P : (mb + 1) * P, :])
             return page
 
+        load_least(0, 0)
+        gather_v(0, 0)
+        gather_v(0, 1)
+        load_w1(0, 1)
+        quantise_w1(0, 0)
+        load_w1(1, 1)
+        deal_w2(0)
+        load_w2(1)
+        gather_v(1, 0)
+        quantise_w1(1, 0)
+        load_least(0, 1)
+        gather_v(1, 1)
+        load_least(1, 0)
+        features_on_vector(0, 0)
+        tab2_sb = [load_words(tab2_words, 0)]
+        quantise_w1(0, 1)
+        tab2_sb.append(load_words(tab2_words, 1))
+        quantise_w1(1, 1)
+        load_least(1, 1)
+        deal_w2(1)
         pages = [load_page(0)]
-        gather_v2(tab2_plane, tab2_sb, idx2)
+        tab2_plane = held([P, T3], U8, "raw_plane")
+        nc.gpsimd.memset(tab2_plane[:].bitcast(I32), 0)
+        load_packed_scales(nc.sync, tab2_plane, tab2_scales)
+        wgo_sb = ring.tile([P, S], F32, name="w1_grouped", align_bytes=64)
+        nc.sync.dma_start(out=wgo_sb[:], in_=wgo)
+        limits = ring.tile([P, 2, 8], F32, name="w1_grouped", align_bytes=64)
+        with nc.allow_non_contiguous_dma("one value of a short vector to each partition"):
+            nc.sync.dma_start(out=limits[:, 0, 0:m_tiles], in_=peer.rearrange("(mb p) -> p mb", p=P))
+            nc.sync.dma_start(out=limits[:, 1, 0:m_tiles], in_=cap.rearrange("(mb p) -> p mb", p=P))
+        features_on_vector(0, 1)
         pages.append(load_page(1))
+        features_on_vector(1, 0)
         pages.append(load_page(2))
-        features(1, 1)
+        gather_v2(tab2_plane, tab2_sb, idx2)
         pages.append(load_page(3))
+        features_on_vector(1, 1)
         for mb in range(m_tiles):
             for jc in range(j_chunks):
                 scores(mb, jc, pages[mb])

@@ -1,6 +1,7 @@
 from contextlib import ExitStack
 
 import concourse.mybir as mybir
+from concourse.masks import make_identity
 
 K, T, S, H, T3, S2, T2 = 1024, 2048, 1024, 1024, 2048, 512, 2048
 FLOPS = 2 * K * H * S * 2 + 2 * H * S2 * S
@@ -42,7 +43,7 @@ def tile_list_league_page_scores_kernel(
             return keep.tile(shape, dtype, name=name, align_bytes=64)
 
         def streamed(shape, dtype):
-            return ring.tile(shape, dtype, name="stream", bufs=6, align_bytes=64)
+            return ring.tile(shape, dtype, name="stream", bufs=5, align_bytes=64)
 
         def load_words(table, a):
             words = streamed([P, table.shape[2]], I32)
@@ -93,12 +94,14 @@ def tile_list_league_page_scores_kernel(
 
         w2_plane_raw = held([P, k_passes, H], U8, "raw_plane")
         nc.gpsimd.memset(w2_plane_raw[:].rearrange("p a c -> p (a c)").bitcast(I32), 0)
-        tab_plane = streamed([P, T], U8)
+        tab_plane = held([P, T], U8, "tab_plane")
         nc.vector.memset(tab_plane[:].bitcast(I32), 0)
         tab_rows = held([P, T], U8, "tab_rows")
         load_packed_scales(nc.sync, tab_rows, tab_scales)
         idx = load_list(offs, "idx")
         tab_sb = [load_words(tab_words, 0)]
+        idx2 = load_list(offs2, "idx2")
+        idx3 = load_list(offs3, "idx3")
         load_w1(0, 0)
         load_w2(0)
         for q in range(QUADS):
@@ -110,8 +113,6 @@ def tile_list_league_page_scores_kernel(
         tab_sb.append(load_words(tab_words, 1))
         gain_sb = held([P, r_passes, PACK], F32, "gain_sb")
         nc.gpsimd.dma_start(out=gain_sb[:], in_=gain.rearrange("(b p t) -> p b t", p=P, t=PACK))
-        idx2 = load_list(offs2, "idx2")
-        idx3 = load_list(offs3, "idx3")
 
         v_plane1 = held([P, S], U8, "v_plane1")
         nc.gpsimd.memset(v_plane1[:].bitcast(I32), 0)
@@ -153,8 +154,8 @@ def tile_list_league_page_scores_kernel(
         def quantise_w1(a, b):
             grouped = ring.tile([P, PACK, P, PACK], BF16, name="w1_grouped", align_bytes=64)
             nc.scalar.copy(
-                out=grouped[:].rearrange("p t m i -> p m i t"),
-                in_=w1_raw[a, b][:].rearrange("p i (m t) -> p m i t", t=PACK),
+                out=grouped[:].rearrange("p (s t) m i -> p s m i t", t=2),
+                in_=w1_raw[a, b][:].rearrange("p i (m s t) -> p s m i t", s=2, t=2),
             )
             codes = held([P, PASS], U32, "w1_codes%d%d" % (a, b))
             plane = held([P, PASS], U8, "w1_plane%d%d" % (a, b))
@@ -203,18 +204,18 @@ def tile_list_league_page_scores_kernel(
 
         def floor_and_round(out_rows, sums, floor_rows):
             nc.vector.tensor_tensor(
-                out=out_rows.rearrange("p (c i) t -> p c t i", i=4),
-                in0=sums.rearrange("p t (c i) -> p c t i", i=4),
-                in1=floor_rows.rearrange("p t (c i) -> p c t i", i=4),
+                out=out_rows.rearrange("p (c i) t -> p c t i", i=2),
+                in0=sums.rearrange("p t (c i) -> p c t i", i=2),
+                in1=floor_rows.rearrange("p t (c i) -> p c t i", i=2),
                 op=ALU.max,
             )
 
         def features_on_vector(b, jc):
             u = ring.tile([P, PACK, NJ], F32, name="u")
             for t in range(PACK):
-                x_ps = psum.tile([P, NJ], F32, name="x_ps", bufs=3)
-                d_ps = psum.tile([P, NJ], F32, name="d_ps", bufs=3)
-                bent = ring.tile([P, NJ], F32, name="bent", bufs=4)
+                x_ps = psum.tile([P, NJ], F32, name="x_ps", bufs=2)
+                d_ps = psum.tile([P, NJ], F32, name="sums", bufs=6)
+                bent = ring.tile([P, NJ], F32, name="bent", bufs=6)
                 products(b, t, jc, x_ps, d_ps, bent)
                 nc.vector.scalar_tensor_tensor(
                     out=u[:, t, :], in0=bent[:], scalar=gain_sb[:, b, t : t + 1], in1=d_ps[:],
@@ -236,7 +237,7 @@ def tile_list_league_page_scores_kernel(
 
         def scores(mb, jc, page):
             peers = slice(mb * P, (mb + 1) * P)
-            e_ps = psum.tile([P, NJ], F32, name="e_ps", bufs=2)
+            e_ps = psum.tile([P, NJ], F32, name="sums", bufs=6)
             for b in range(r_passes):
                 nc.tensor.matmul_mx(
                     out=e_ps[:],
@@ -251,7 +252,7 @@ def tile_list_league_page_scores_kernel(
             nc.scalar.copy(out=e_sb[:], in_=e_ps[:])
             capped = ring.tile([P, NJ], F32, name="capped")
             nc.vector.tensor_scalar(
-                out=capped[:], in0=e_sb[:], scalar1=limits[:, 0, mb : mb + 1], scalar2=limits[:, 1, mb : mb + 1],
+                out=capped[:], in0=e_sb[:], scalar1=limits[:, mb : mb + 1], scalar2=limits[:, m_tiles + mb : m_tiles + mb + 1],
                 op0=ALU.mult, op1=ALU.min,
             )
             nc.vector.tensor_tensor(
@@ -266,43 +267,49 @@ def tile_list_league_page_scores_kernel(
             nc.sync.dma_start(out=page[:], in_=page1[mb * P : (mb + 1) * P, :])
             return page
 
-        load_least(0, 0)
         gather_v(0, 0)
         gather_v(0, 1)
-        load_w1(0, 1)
+        load_least(0, 0)
         quantise_w1(0, 0)
-        load_w1(1, 1)
+        load_w1(0, 1)
         deal_w2(0)
-        load_w2(1)
+        load_w1(1, 1)
         gather_v(1, 0)
         quantise_w1(1, 0)
-        load_least(0, 1)
+        load_w2(1)
         gather_v(1, 1)
-        load_least(1, 0)
+        load_least(0, 1)
+        identity = held([P, P], F32, "identity")
+        make_identity(nc, identity[:])
         features_on_vector(0, 0)
-        tab2_sb = [load_words(tab2_words, 0)]
+        load_least(1, 0)
         quantise_w1(0, 1)
-        tab2_sb.append(load_words(tab2_words, 1))
+        tab2_sb = [load_words(tab2_words, 0)]
         quantise_w1(1, 1)
         load_least(1, 1)
         deal_w2(1)
-        pages = [load_page(0)]
+        tab2_sb.append(load_words(tab2_words, 1))
         tab2_plane = held([P, T3], U8, "raw_plane")
         nc.gpsimd.memset(tab2_plane[:].bitcast(I32), 0)
         load_packed_scales(nc.sync, tab2_plane, tab2_scales)
+        limit_rows = ring.tile([P, P], F32, name="w1_grouped", align_bytes=64)
+        nc.gpsimd.memset(limit_rows[:], 0.0)
+        nc.sync.dma_start(out=limit_rows[0:m_tiles, :], in_=peer.rearrange("(mb p) -> mb p", p=P))
+        nc.sync.dma_start(out=limit_rows[m_tiles : 2 * m_tiles, :], in_=cap.rearrange("(mb p) -> mb p", p=P))
         wgo_sb = ring.tile([P, S], F32, name="w1_grouped", align_bytes=64)
         nc.sync.dma_start(out=wgo_sb[:], in_=wgo)
-        limits = ring.tile([P, 2, 8], F32, name="w1_grouped", align_bytes=64)
-        with nc.allow_non_contiguous_dma("one value of a short vector to each partition"):
-            nc.sync.dma_start(out=limits[:, 0, 0:m_tiles], in_=peer.rearrange("(mb p) -> p mb", p=P))
-            nc.sync.dma_start(out=limits[:, 1, 0:m_tiles], in_=cap.rearrange("(mb p) -> p mb", p=P))
         features_on_vector(0, 1)
-        pages.append(load_page(1))
+        pages = [load_page(0)]
         features_on_vector(1, 0)
-        pages.append(load_page(2))
+        pages.append(load_page(1))
+        limits_ps = psum.tile([P, P], F32, name="sums", bufs=6)
+        nc.tensor.transpose(limits_ps[:], limit_rows[:], identity[:])
+        limits = held([P, 2 * m_tiles], F32, "limits")
+        nc.scalar.copy(out=limits[:], in_=limits_ps[:, 0 : 2 * m_tiles])
         gather_v2(tab2_plane, tab2_sb, idx2)
-        pages.append(load_page(3))
+        pages.append(load_page(2))
         features_on_vector(1, 1)
+        pages.append(load_page(3))
         for mb in range(m_tiles):
             for jc in range(j_chunks):
                 scores(mb, jc, pages[mb])

from contextlib import ExitStack

import concourse.mybir as mybir
from concourse.masks import make_identity

K, T, S, H, T3, S2, T2 = 1024, 2048, 1024, 1024, 2048, 512, 2048
FLOPS = 2 * K * H * S * 2 + 2 * H * S2 * S

F32 = mybir.dt.float32
BF16 = mybir.dt.bfloat16
I32 = mybir.dt.int32
U32 = mybir.dt.uint32
U16 = mybir.dt.uint16
U8 = mybir.dt.uint8
FP8X4 = mybir.dt.float8_e4m3fn_x4
FP4X4 = mybir.dt.float4_e2m1fn_x4
ALU = mybir.AluOpType
ACT = mybir.ActivationFunctionType

P = 128
PACK = 4
PASS = P * PACK
QUADS = 4
NJ = 512


def tile_list_league_page_scores_kernel(
    tc, tab_words, tab_scales, offs, tab2_words, tab2_scales, offs2, offs3,
    w1, w2_words, w2_scales, gain, least, peer, cap, wgo, page1, out,
):
    nc = tc.nc
    k_passes = K // PASS
    r_passes = H // PASS
    j_chunks = S // NJ
    m_tiles = S2 // P

    with ExitStack() as ctx:
        keep = ctx.enter_context(tc.tile_pool(name="keep", bufs=1))
        ring = ctx.enter_context(tc.tile_pool(name="ring", bufs=2))
        psum = ctx.enter_context(tc.psum_pool(name="psum", bufs=1))

        def held(shape, dtype, name):
            return keep.tile(shape, dtype, name=name, align_bytes=64)

        def streamed(shape, dtype):
            return ring.tile(shape, dtype, name="stream", bufs=5, align_bytes=64)

        def load_words(table, a):
            words = streamed([P, table.shape[2]], I32)
            nc.sync.dma_start(out=words[:], in_=table[a].rearrange("p t i -> p (t i)").bitcast(I32))
            return words

        def load_packed_scales(queue, plane, scales):
            for q in range(QUADS):
                queue.dma_start(
                    out=plane[32 * q : 32 * q + 8, :].bitcast(I32),
                    in_=scales[:, 4 * q : 4 * q + 4, :].bitcast(I32),
                )

        w1_raw = {}

        def load_w1(a, b):
            raw = streamed([P, PACK, PASS], F32)
            nc.sync.dma_start(
                out=raw[:],
                in_=w1[a * PASS : (a + 1) * PASS, b * PASS : (b + 1) * PASS].rearrange("(p i) c -> p i c", i=PACK),
            )
            w1_raw[a, b] = raw

        w2_raw = {}

        def load_w2(b):
            raw = streamed([P, k_passes, PASS // 2], I32)
            nc.sync.dma_start(
                out=raw[:],
                in_=w2_words[:, :, 2 * b * PASS : 2 * (b + 1) * PASS].rearrange("a p c -> p a c").bitcast(I32),
            )
            w2_raw[b] = raw

        least_sb = {}

        def load_least(b, jc):
            rows = streamed([P, PACK, NJ], F32)
            nc.sync.dma_start(
                out=rows[:],
                in_=least[b * PASS : (b + 1) * PASS, jc * NJ : (jc + 1) * NJ].rearrange("(p t) j -> p t j", t=PACK),
            )
            least_sb[b, jc] = rows

        def load_list(source, name):
            entries = held(list(source.shape), U16, name)
            nc.sync.dma_start(out=entries[:], in_=source)
            return entries

        w2_plane_raw = held([P, k_passes, H], U8, "raw_plane")
        nc.gpsimd.memset(w2_plane_raw[:].rearrange("p a c -> p (a c)").bitcast(I32), 0)
        tab_plane = held([P, T], U8, "tab_plane")
        nc.vector.memset(tab_plane[:].bitcast(I32), 0)
        tab_rows = held([P, T], U8, "tab_rows")
        load_packed_scales(nc.sync, tab_rows, tab_scales)
        idx = load_list(offs, "idx")
        tab_sb = [load_words(tab_words, 0)]
        idx2 = load_list(offs2, "idx2")
        idx3 = load_list(offs3, "idx3")
        load_w1(0, 0)
        load_w2(0)
        for q in range(QUADS):
            nc.sync.dma_start(
                out=w2_plane_raw[32 * q : 32 * q + 4, :, :].bitcast(I32),
                in_=w2_scales[:, 4 * q : 4 * q + 4, :].rearrange("a r c -> r a c").bitcast(I32),
            )
        load_w1(1, 0)
        tab_sb.append(load_words(tab_words, 1))
        gain_sb = held([P, r_passes, PACK], F32, "gain_sb")
        nc.gpsimd.dma_start(out=gain_sb[:], in_=gain.rearrange("(b p t) -> p b t", p=P, t=PACK))

        v_plane1 = held([P, S], U8, "v_plane1")
        nc.gpsimd.memset(v_plane1[:].bitcast(I32), 0)
        for q in range(QUADS):
            live = slice(32 * q, 32 * q + 8)
            nc.vector.tensor_copy(out=tab_plane[live, :].bitcast(I32), in_=tab_rows[live, :].bitcast(I32))
        v_plane = held([P, S], U8, "v_plane")
        nc.vector.tensor_copy(out=v_plane[:], in_=tab_plane[:].indirect(idx[:]))
        nc.sync.dma_start(out=v_plane1[0:100, :].bitcast(I32), in_=v_plane[4:104, :].bitcast(I32))

        v_codes = {}

        def gather_v(a, jc):
            codes = held([P, NJ], U32, "v_codes%d%d" % (a, jc))
            cols = slice(jc * NJ // 16, (jc + 1) * NJ // 16)
            nc.vector.tensor_copy(out=codes[:], in_=tab_sb[a][:].bitcast(U32).indirect(idx[:, cols]))
            v_codes[a, jc] = codes

        w2_codes = {}
        w2_plane = {}

        def deal_w2(b):
            codes = held([P, k_passes, PACK, P], U16, "w2_codes%d" % b)
            plane = held([P, k_passes, PACK, P], U8, "w2_plane%d" % b)
            nc.vector.tensor_copy(
                out=codes[:],
                in_=w2_raw[b][:].rearrange("p a c -> p (a c)").bitcast(U16).rearrange("p (a m t) -> p a t m", t=PACK, m=P),
            )
            nc.vector.tensor_copy(
                out=plane[:],
                in_=w2_plane_raw[:, :, b * PASS : (b + 1) * PASS].rearrange("p a (m t) -> p a t m", t=PACK),
            )
            w2_codes[b] = codes
            w2_plane[b] = plane

        w1_codes = {}
        w1_plane = {}

        def quantise_w1(a, b):
            grouped = ring.tile([P, PACK, P, PACK], BF16, name="w1_grouped", align_bytes=64)
            nc.scalar.copy(
                out=grouped[:].rearrange("p (s t) m i -> p s m i t", t=2),
                in_=w1_raw[a, b][:].rearrange("p i (m s t) -> p s m i t", s=2, t=2),
            )
            codes = held([P, PASS], U32, "w1_codes%d%d" % (a, b))
            plane = held([P, PASS], U8, "w1_plane%d%d" % (a, b))
            nc.vector.quantize_mx(
                out=codes[:].bitcast(FP8X4), scales=plane[:], in_=grouped[:].rearrange("p t m i -> p (t m i)")
            )
            w1_codes[a, b] = codes
            w1_plane[a, b] = plane

        h_codes = {}
        h_plane = {}

        def products(b, t, jc, x_ps, d_ps, bent):
            cols = slice(jc * NJ, (jc + 1) * NJ)
            ch = slice(t * P, (t + 1) * P)
            for a in range(k_passes):
                nc.tensor.matmul_mx(
                    out=x_ps[:],
                    lhsT=w1_codes[a, b][:, ch].bitcast(FP8X4),
                    lhsT_scale=w1_plane[a, b][:, ch],
                    rhs=v_codes[a, jc][:].bitcast(FP8X4),
                    rhs_scale=v_plane[4 * a : P, cols],
                    start=(a == 0),
                    stop=(a == k_passes - 1),
                )
            for a in range(k_passes):
                nc.tensor.matmul_mx(
                    out=d_ps[:],
                    lhsT=w2_codes[b][:, a, t, :].bitcast(FP4X4),
                    lhsT_scale=w2_plane[b][:, a, t, :],
                    rhs=v_codes[a, jc][:].bitcast(FP8X4),
                    rhs_scale=(v_plane, v_plane1)[a][:, cols],
                    start=(a == 0),
                    stop=(a == k_passes - 1),
                )
            nc.scalar.activation(out=bent[:], in_=x_ps[:], func=ACT.Tanh)

        def quantise_h(b, jc, grouped):
            codes = held([P, NJ], U32, "h_codes%d%d" % (b, jc))
            plane = held([P, NJ], U8, "h_plane%d%d" % (b, jc))
            nc.vector.quantize_mx(
                out=codes[:].bitcast(FP8X4), scales=plane[:], in_=grouped[:].rearrange("p j t -> p (j t)")
            )
            h_codes[b, jc] = codes
            h_plane[b, jc] = plane

        def floor_and_round(out_rows, sums, floor_rows):
            nc.vector.tensor_tensor(
                out=out_rows.rearrange("p (c i) t -> p c t i", i=2),
                in0=sums.rearrange("p t (c i) -> p c t i", i=2),
                in1=floor_rows.rearrange("p t (c i) -> p c t i", i=2),
                op=ALU.max,
            )

        def features_on_vector(b, jc):
            u = ring.tile([P, PACK, NJ], F32, name="u")
            for t in range(PACK):
                x_ps = psum.tile([P, NJ], F32, name="x_ps", bufs=2)
                d_ps = psum.tile([P, NJ], F32, name="sums", bufs=6)
                bent = ring.tile([P, NJ], F32, name="bent", bufs=6)
                products(b, t, jc, x_ps, d_ps, bent)
                nc.vector.scalar_tensor_tensor(
                    out=u[:, t, :], in0=bent[:], scalar=gain_sb[:, b, t : t + 1], in1=d_ps[:],
                    op0=ALU.mult, op1=ALU.add,
                )
            grouped = ring.tile([P, NJ, PACK], BF16, name="h_grouped", align_bytes=64)
            floor_and_round(grouped[:], u[:], least_sb[b, jc][:])
            quantise_h(b, jc, grouped)

        v2_codes = []
        v2_plane = held([P, S2], U8, "v2_plane")

        def gather_v2(tab2_plane, tab2_sb, idx2):
            nc.vector.tensor_copy(out=v2_plane[:], in_=tab2_plane[:].indirect(idx2[:]))
            for b in range(r_passes):
                codes = held([P, S2], U32, "v2_codes%d" % b)
                nc.vector.tensor_copy(out=codes[:], in_=tab2_sb[b][:].bitcast(U32).indirect(idx2[:]))
                v2_codes.append(codes)

        def scores(mb, jc, page):
            peers = slice(mb * P, (mb + 1) * P)
            e_ps = psum.tile([P, NJ], F32, name="sums", bufs=6)
            for b in range(r_passes):
                nc.tensor.matmul_mx(
                    out=e_ps[:],
                    lhsT=v2_codes[b][:, peers].bitcast(FP8X4),
                    lhsT_scale=v2_plane[4 * b : P, peers],
                    rhs=h_codes[b, jc][:].bitcast(FP8X4),
                    rhs_scale=h_plane[b, jc][:],
                    start=(b == 0),
                    stop=(b == r_passes - 1),
                )
            e_sb = ring.tile([P, NJ], F32, name="e_sb", bufs=8)
            nc.scalar.copy(out=e_sb[:], in_=e_ps[:])
            capped = ring.tile([P, NJ], F32, name="capped")
            nc.vector.tensor_scalar(
                out=capped[:], in0=e_sb[:], scalar1=limits[:, mb : mb + 1], scalar2=limits[:, m_tiles + mb : m_tiles + mb + 1],
                op0=ALU.mult, op1=ALU.min,
            )
            nc.vector.tensor_tensor(
                out=page[:].indirect(idx3[:, jc * NJ // 16 : (jc + 1) * NJ // 16]),
                in0=capped[:],
                in1=wgo_sb[:, jc * NJ : (jc + 1) * NJ],
                op=ALU.mult,
            )

        def load_page(mb):
            page = streamed([P, T2], F32)
            nc.sync.dma_start(out=page[:], in_=page1[mb * P : (mb + 1) * P, :])
            return page

        gather_v(0, 0)
        gather_v(0, 1)
        load_least(0, 0)
        quantise_w1(0, 0)
        load_w1(0, 1)
        deal_w2(0)
        load_w1(1, 1)
        gather_v(1, 0)
        quantise_w1(1, 0)
        load_w2(1)
        gather_v(1, 1)
        load_least(0, 1)
        identity = held([P, P], F32, "identity")
        make_identity(nc, identity[:])
        features_on_vector(0, 0)
        load_least(1, 0)
        quantise_w1(0, 1)
        tab2_sb = [load_words(tab2_words, 0)]
        quantise_w1(1, 1)
        load_least(1, 1)
        deal_w2(1)
        tab2_sb.append(load_words(tab2_words, 1))
        tab2_plane = held([P, T3], U8, "raw_plane")
        nc.gpsimd.memset(tab2_plane[:].bitcast(I32), 0)
        load_packed_scales(nc.sync, tab2_plane, tab2_scales)
        limit_rows = ring.tile([P, P], F32, name="w1_grouped", align_bytes=64)
        nc.gpsimd.memset(limit_rows[:], 0.0)
        nc.sync.dma_start(out=limit_rows[0:m_tiles, :], in_=peer.rearrange("(mb p) -> mb p", p=P))
        nc.sync.dma_start(out=limit_rows[m_tiles : 2 * m_tiles, :], in_=cap.rearrange("(mb p) -> mb p", p=P))
        wgo_sb = ring.tile([P, S], F32, name="w1_grouped", align_bytes=64)
        nc.sync.dma_start(out=wgo_sb[:], in_=wgo)
        features_on_vector(0, 1)
        pages = [load_page(0)]
        features_on_vector(1, 0)
        pages.append(load_page(1))
        limits_ps = psum.tile([P, P], F32, name="sums", bufs=6)
        nc.tensor.transpose(limits_ps[:], limit_rows[:], identity[:])
        limits = held([P, 2 * m_tiles], F32, "limits")
        nc.scalar.copy(out=limits[:], in_=limits_ps[:, 0 : 2 * m_tiles])
        gather_v2(tab2_plane, tab2_sb, idx2)
        pages.append(load_page(2))
        features_on_vector(1, 1)
        pages.append(load_page(3))
        for mb in range(m_tiles):
            for jc in range(j_chunks):
                scores(mb, jc, pages[mb])
            nc.sync.dma_start(out=out[mb * P : (mb + 1) * P, :], in_=pages[mb][:])
